import numpy as np
import ml_dtypes


def mxq(x, axis, fmt="e4m3"):
    dtype, down = {"e4m3": (ml_dtypes.float8_e4m3fn, 7), "e5m2": (ml_dtypes.float8_e5m2, 14)}[fmt]
    v = np.moveaxis(np.asarray(x, np.float32).astype(ml_dtypes.bfloat16).astype(np.float64), axis, -1)
    blocks = v.reshape(v.shape[:-1] + (-1, 32))
    amax = np.abs(blocks).max(-1, keepdims=True)
    byte = np.maximum(np.where(amax > 0, np.frexp(amax)[1] - 1 + 127, 0) - down, 1)
    scale = np.exp2(byte - 127.0)
    codes = (blocks / scale).astype(np.float32).astype(dtype).astype(np.float64)
    return np.moveaxis((codes * scale).reshape(v.shape), -1, axis)


WIDE = False


def mx_kscale(k):
    if not WIDE:
        return np.ones(k)
    levels = np.array([10, -10, 5, -5, 0])
    if k % 512:
        return np.exp2(np.random.permutation(np.resize(levels, k // 32))).repeat(32)
    a = np.empty((k // 512, 16))
    for p in range(k // 512):
        a[p, :8] = np.random.permutation(np.resize(levels, 8))
        for g in range(8):
            far = levels[np.abs(levels - a[p, g]) >= 10]
            a[p, g + 8] = far[np.random.randint(len(far))]
    return np.exp2(a.ravel()).repeat(32)


BF16 = ml_dtypes.bfloat16


def bf(x):
    return np.asarray(x, np.float32).astype(BF16)


def f64(x):
    return np.asarray(x).astype(np.float64)


E2M1 = np.array([0.0, 0.5, 1.0, 1.5, 2.0, 3.0, 4.0, 6.0, -0.0, -0.5, -1.0, -1.5, -2.0, -3.0, -4.0, -6.0])


def pack_weight(w, fmt):
    k, n = w.shape
    w = f64(bf(w)).reshape(k // 32, 32, n)
    amax = np.abs(w).max(1)
    if fmt == "e4m3":
        byte = np.frexp(amax)[1] - 1 + 127 - 7
    else:
        mant, ex = np.frexp(amax / 6.0)
        byte = np.where(mant > 0.5, ex, ex - 1) + 127
    byte = np.clip(np.where(amax > 0, byte, 1), 1, 254)
    scaled = (w * np.exp2(127.0 - byte)[:, None, :]).reshape(k, n).astype(np.float32)
    by_word = np.ascontiguousarray(scaled.reshape(k // 512, 128, 4, n).transpose(0, 1, 3, 2))
    if fmt == "e4m3":
        words = by_word.astype(ml_dtypes.float8_e4m3fn).view(np.uint8)
    else:
        c = by_word.astype(ml_dtypes.float4_e2m1fn).view(np.uint8) & 0xF
        words = c[..., 0::2] | (c[..., 1::2] << 4)
    return np.ascontiguousarray(words), np.ascontiguousarray(byte.astype(np.uint8).reshape(k // 512, 16, n))


def unpack_weight(words, scales, fmt):
    g, p, n, _ = words.shape
    if fmt == "e4m3":
        vals = np.ascontiguousarray(words).view(ml_dtypes.float8_e4m3fn).astype(np.float64)
    else:
        nib = np.empty((g, p, n, 4), np.uint8)
        nib[..., 0::2] = words & 0xF
        nib[..., 1::2] = words >> 4
        vals = E2M1[nib]
    vals = vals * np.repeat(np.exp2(scales.astype(np.float64) - 127.0), 8, axis=1)[..., None]
    return vals.transpose(0, 1, 3, 2).reshape(g * 512, n)
def pack4(w):
    words, scales = pack_weight(w, "e2m1")
    return words.reshape(words.shape[0], 128, -1), scales


def unpack4(words, scales):
    return unpack_weight(words.reshape(words.shape[0], 128, -1, 2), scales, "e2m1")


B, P, M, C, R, E = 128, 8, 1024, 4096, 1024, 8192


def silu(v):
    return v / (1.0 + np.exp(-v))


def sigmoid(v):
    return 1.0 / (1.0 + np.exp(-v))


def setup_inputs():
    s, t = mx_kscale(C), mx_kscale(R)
    f = np.random.standard_normal((M, C))
    x_words, x_scales = pack4((f * s).T)
    w1_words, w1_scales = pack4(np.random.standard_normal((C, R)) / np.sqrt(C) / s[:, None])
    w2_words, w2_scales = pack4(np.random.standard_normal((R, E)) / np.sqrt(R) / t[:, None])
    return {"x_words": x_words, "x_scales": x_scales,
            "w1_words": w1_words, "w1_scales": w1_scales,
            "b1": bf(0.3 * np.random.standard_normal(R)),
            "gain_mean": bf((1.0 + 0.3 * np.random.standard_normal(R)) * t),
            "gain_max": bf((1.0 + 0.3 * np.random.standard_normal(R)) * t),
            "w2_words": w2_words, "w2_scales": w2_scales,
            "b2": bf(0.3 * np.random.standard_normal(E)),
            "y": bf(f.reshape(B, P, C))}


def reference(x_words, x_scales, w1_words, w1_scales, b1, gain_mean, gain_max, w2_words, w2_scales, b2, y):
    h = unpack4(x_words, x_scales).T @ unpack4(w1_words, w1_scales)
    a = silu(h + f64(b1)).reshape(B, P, R)
    u = f64(gain_mean) * a.mean(axis=1) + f64(gain_max) * a.max(axis=1)
    z = (mxq(u, 1, "e4m3") @ unpack4(w2_words, w2_scales)) + f64(b2)
    gate = sigmoid(z[:, :C])
    shift = z[:, C:]
    return f64(y).reshape(B, P, C) * gate[:, None, :] + shift[:, None, :]

@@ -1,0 +1,356 @@
+from contextlib import ExitStack
+
+import concourse.mybir as mybir
+from concourse.masks import make_identity
+
+B, P, M, C, R, E = 128, 8, 1024, 4096, 1024, 8192
+FLOPS = 2 * M * C * R + 2 * B * R * E
+
+F32 = mybir.dt.float32
+BF16 = mybir.dt.bfloat16
+U32 = mybir.dt.uint32
+I32 = mybir.dt.int32
+U8 = mybir.dt.uint8
+FP8X4 = mybir.dt.float8_e4m3fn_x4
+FP4X4 = mybir.dt.float4_e2m1fn_x4
+ACT = mybir.ActivationFunctionType
+ALU = mybir.AluOpType
+AX = mybir.AxisListType
+
+W_V = (384, 128, 128, 128, 128, 128, 192, 192, 176, 176, 176, 176, 176, 176, 176, 176)
+
+
+def tile_squeeze_excite_shift_f2_kernel(
+    tc, x_words, x_scales, w1_words, w1_scales, b1, gain_mean, gain_max,
+    w2_words, w2_scales, b2, y, out,
+):
+    nc = tc.nc
+    with ExitStack() as ctx:
+        keep = ctx.enter_context(tc.tile_pool(name="keep", bufs=1))
+        work = ctx.enter_context(tc.tile_pool(name="work", bufs=2))
+        psum = ctx.enter_context(tc.psum_pool(name="psum", bufs=1))
+        ctx.enter_context(tc.manual_schedule())
+
+        def bank(i, shape=(128, 512), dtype=F32):
+            return psum.tile(list(shape), dtype, name="bank%d" % i, tag="bank%d" % i)
+
+        xw = keep.tile([128, 8, 2048], U8, name="xw", align_bytes=64)
+        xs = [keep.tile([128, 8, 512], U8, name="xs%d" % h, align_bytes=64) for h in range(2)]
+        w1 = keep.tile([128, 8, 2048], U8, name="w1", align_bytes=64)
+        w1s = [keep.tile([128, 8, 512], U8, name="w1s%d" % g2, align_bytes=64) for g2 in range(2)]
+        w2 = keep.tile([128, 2, 16384], U8, name="w2", align_bytes=64)
+        w2s = keep.tile([128, 2, 8192], U8, name="w2s", align_bytes=64)
+        ys = [[keep.tile([128, 4, 1024], BF16, name="y%d_%d" % (h, q), align_bytes=64) for q in range(4)] for h in range(2)]
+        idf = keep.tile([128, 128], F32, name="idf", align_bytes=64)
+        idb = keep.tile([128, 128], BF16, name="idb", align_bytes=64)
+        sel = keep.tile([128, 4, 224], BF16, name="sel", align_bytes=64)
+        vr = keep.tile([128, 128], BF16, name="vr", align_bytes=64)
+        cst = keep.tile([128, 88], F32, name="cst", align_bytes=64)
+        one = keep.tile([128, 1], F32, name="one")
+        dummy = keep.tile([128, 1], F32, name="dummy")
+
+        nc.gpsimd.memset(dummy[:], 0.0)
+        nc.scalar.activation(out=dummy[:], in_=dummy[:], func=ACT.Silu)
+
+        def zero(eng, t):
+            eng.memset(t.rearrange("p g n -> p (g n)").bitcast(I32), 0)
+
+        nc.vector.memset(vr[64:128, :], 0.0)
+        zero(nc.vector, xs[0][:])
+        zero(nc.vector, w1s[0][:])
+        zero(nc.vector, w1s[1][:])
+        zero(nc.vector, xs[1][:])
+        make_identity(nc, idb[:])
+        zero(nc.gpsimd, w2s[:])
+        nc.gpsimd.memset(one[:], 1.0)
+        make_identity(nc, idf[:])
+        nc.vector.memset(sel[:], 0.0)
+        nc.vector.tensor_copy(out=sel[:, :, 96:128], in_=idb[:].rearrange("p (i t) -> p t i", t=4))
+
+        def load(dst, src):
+            nc.sync.dma_start(out=dst, in_=src)
+
+        def load_words(dst, src, half, a, b):
+            cols = slice(half * 1024, (half + 1) * 1024)
+            load(dst[:, a:b, cols].bitcast(I32), src[a:b, :, cols].rearrange("g p n -> p g n").bitcast(I32))
+
+        def load_scales(dst, src):
+            for q in range(4):
+                load(dst[32 * q:32 * q + 4, :, :].bitcast(I32),
+                     src[:, 4 * q:4 * q + 4, :].rearrange("g r n -> r g n").bitcast(I32))
+
+        def load_w2(part, q):
+            c0 = part * 8192 + q * 2048
+            load(w2[:, :, c0:c0 + 2048].bitcast(I32),
+                 w2_words[:, :, c0:c0 + 2048].rearrange("g p n -> p g n").bitcast(I32))
+
+        def rows(t, h):
+            return t[64 * h:64 * h + 64].rearrange("i (r j) c -> (i r) j c", r=2)
+
+        def load_y(h, q):
+            load(ys[h][q][:], rows(y, h)[:, :, q * 1024:(q + 1) * 1024])
+
+        load_words(xw, x_words, 0, 0, 2)
+        load_words(w1, w1_words, 0, 0, 2)
+        load_scales(xs[0], x_scales[:, :, 0:512])
+        load_scales(w1s[0], w1_scales[:, :, 0:512])
+        load_words(w1, w1_words, 0, 2, 5)
+        load_words(xw, x_words, 0, 2, 5)
+        load_words(w1, w1_words, 0, 5, 8)
+        load_words(xw, x_words, 0, 5, 8)
+        load(vr[0:64, :], b2.rearrange("(t p) -> t p", p=128))
+        for i, v in enumerate((b1, gain_mean, gain_max)):
+            load(vr[64 + 8 * i:72 + 8 * i, :], v.rearrange("(t p) -> t p", p=128))
+        load_words(w1, w1_words, 1, 0, 8)
+        load_scales(w1s[1], w1_scales[:, :, 512:1024])
+        load_words(xw, x_words, 1, 0, 8)
+        load_scales(xs[1], x_scales[:, :, 512:1024])
+        load_scales(w2s, w2_scales)
+        for q in range(4):
+            load_w2(0, q)
+            load_w2(1, q)
+            load_y(0, q)
+        for q in range(4):
+            load_y(1, q)
+
+        def mm1(ps, h, g2, t, g):
+            col = g2 * 512 + t * 128
+            nc.tensor.matmul_mx(
+                out=ps[:],
+                lhsT=w1[:, g, 2 * col:2 * col + 256].bitcast(FP4X4),
+                lhsT_scale=w1s[g2][:, g, t * 128:(t + 1) * 128],
+                rhs=xw[:, g, h * 1024:(h + 1) * 1024].bitcast(FP4X4),
+                rhs_scale=xs[h][:, g, :],
+                start=(g == 0), stop=(g == 7))
+
+        acc = {}
+
+        def begin_group(h, g2):
+            acc[(h, g2)] = [work.tile([128, 4, 64], F32, name=s, tag=s) for s in ("asum", "amax", "usum", "umax")]
+
+        def silu(ps, h, g2, t):
+            a = work.tile([128, 512], F32, name="a", tag="a", bufs=4)
+            r = 64 + 4 * g2 + t
+            nc.scalar.activation(out=a[:], in_=ps[:], func=ACT.Silu, bias=cst[:, r:r + 1])
+            return a
+
+        def reduce(a, h, g2, t):
+            asum, amax, usum, umax = acc[(h, g2)]
+            av = a[:].rearrange("p (i j) -> p i j", j=8)
+            nc.vector.tensor_reduce(out=asum[:, t, :], in_=av, axis=AX.X, op=ALU.add)
+            nc.vector.tensor_reduce(out=amax[:, t, :], in_=av, axis=AX.X, op=ALU.max)
+
+        def scale(h, g2, t):
+            asum, amax, usum, umax = acc[(h, g2)]
+            for src, dst, r in ((asum, usum, 72), (amax, umax, 80)):
+                r = r + 4 * g2 + t
+                nc.scalar.activation(out=dst[:, t, :], in_=src[:, t, :], func=ACT.Copy, scale=cst[:, r:r + 1])
+
+        def group_add(h, g2):
+            asum, amax, usum, umax = acc[(h, g2)]
+            un = work.tile([128, 4, 64], BF16, name="un", tag="un", align_bytes=64)
+            nc.vector.tensor_tensor(out=un[:], in0=usum[:], in1=umax[:], op=ALU.add)
+            return un
+
+        ring = [0]
+
+        def next_bank(shape=(128, 512)):
+            ring[0] += 1
+            return bank((ring[0] - 1) % 4, shape)
+
+        def group_permute(un):
+            ps = next_bank((128, 4, 64))
+            for t in range(4):
+                for s in range(4):
+                    nc.tensor.matmul(ps[:, t, :], lhsT=sel[:, t, 96 - 32 * s:224 - 32 * s], rhs=un[:, s, :],
+                                     start=(s == 0), stop=(s == 3))
+            return ps
+
+        codes = {}
+
+        def group_quant(h, g2, ps):
+            ub = work.tile([128, 64, 2, 4], BF16, name="ub", tag="ub", align_bytes=64)
+            nc.scalar.activation(out=ub[:], in_=ps[:].rearrange("p t i -> p i t").unsqueeze(2).to_broadcast([128, 64, 2, 4]), func=ACT.Copy)
+            uc = keep.tile([128, 128], U32, name="uc%d%d" % (h, g2), align_bytes=64)
+            us = keep.tile([128, 128], U8, name="us%d%d" % (h, g2), align_bytes=64)
+            nc.vector.quantize_mx(out=uc[:].bitcast(FP8X4), scales=us[:], in_=ub[:].rearrange("p i r t -> p (i r t)"))
+            codes[(h, g2)] = (uc, us)
+
+        def zmm(h, n):
+            zs = []
+            for part in range(2):
+                z = next_bank()
+                for ct in range(4):
+                    col = part * 4096 + n * 512 + ct * 128
+                    for g2 in range(2):
+                        uc, us = codes[(h, g2)]
+                        nc.tensor.matmul_mx(
+                            out=z[:, ct * 128:(ct + 1) * 128],
+                            lhsT=w2[:, g2, 2 * col:2 * col + 256].bitcast(FP4X4),
+                            lhsT_scale=w2s[:, g2, col:col + 128],
+                            rhs=uc[:].bitcast(FP8X4),
+                            rhs_scale=us[:],
+                            start=(g2 == 0), stop=(g2 == 1))
+                zs.append(z)
+            return zs
+
+        def evac(zs, n, part):
+            r = work.tile([128, 4, 128], F32, name="zt%d" % part, tag="zt%d" % part, align_bytes=64)
+            for ct in range(4):
+                j = 32 * part + 4 * n + ct
+                if part == 0:
+                    nc.scalar.activation(out=r[:, ct, :], in_=zs[0][:, ct * 128:(ct + 1) * 128], func=ACT.Tanh,
+                                         bias=cst[:, j:j + 1], scale=0.5)
+                else:
+                    nc.scalar.activation(out=r[:, ct, :], in_=zs[1][:, ct * 128:(ct + 1) * 128], func=ACT.Identity,
+                                         bias=cst[:, j:j + 1])
+            return r
+
+        def turn(gs, n):
+            res = []
+            for part in range(2):
+                b = bank(4 + 2 * part + n % 2)
+                for ct in range(4):
+                    nc.tensor.transpose(b[:, ct * 128:(ct + 1) * 128], gs[part][:, ct, :], idf[:])
+                res.append(b)
+            return res
+
+        def gate_copy(gh, h, n):
+            w = W_V[8 * h + n]
+            gs = work.tile([128, 512], F32, name="gs", tag="gs", bufs=3, align_bytes=64)
+            nc.scalar.activation(out=gs[:, w:512], in_=gh[0][:, w:512], func=ACT.Identity, bias=one[:])
+            return gs
+
+        def product(gh, gs, h, n):
+            o = work.tile([128, 4, 512], F32, name="o", tag="o", bufs=4, align_bytes=64)
+            w = W_V[8 * h + n]
+            c0 = (n % 2) * 512
+            yt = ys[h][n // 2]
+            nc.gpsimd.tensor_tensor(out=o[:, :, w:512], in0=yt[:, :, c0 + w:c0 + 512],
+                                    in1=gs[:, w:512].unsqueeze(1).to_broadcast([128, 4, 512 - w]), op=ALU.mult)
+            nc.vector.scalar_tensor_tensor(
+                out=o[:, :, 0:w], in0=gh[0][:, 0:w].unsqueeze(1).to_broadcast([128, 4, w]), scalar=1.0,
+                in1=yt[:, :, c0:c0 + w], op0=ALU.add, op1=ALU.mult)
+            return o
+
+        def add_store(o, gh, h, n, parts=1):
+            s = 4 // parts
+            for j in range(0, 4, s):
+                sh = gh[1][:].unsqueeze(1).to_broadcast([128, s, 512])
+                nc.vector.scalar_tensor_tensor(out=o[:, j:j + s, :], in0=o[:, j:j + s, :], scalar=0.5, in1=sh,
+                                               op0=ALU.mult, op1=ALU.add)
+                nc.sync.dma_start(out=rows(out, h)[:, j:j + s, n * 512:(n + 1) * 512], in_=o[:, j:j + s, :])
+
+        first = [bank(t) for t in range(4)]
+        for g in range(8):
+            for t in range(4):
+                mm1(first[t], 0, 0, t, g)
+            if g == 5:
+                bt = bank(7, (128, 128), BF16)
+                nc.tensor.transpose(bt[:], vr[:], idb[:])
+                nc.vector.tensor_copy(out=cst[:], in_=bt[:, 0:88])
+                nc.vector.tensor_scalar(out=cst[:, 0:32], in0=cst[:, 0:32], scalar1=0.5, scalar2=None, op0=ALU.mult)
+                nc.vector.tensor_scalar(out=cst[:, 72:80], in0=cst[:, 72:80], scalar1=0.125, scalar2=None, op0=ALU.mult)
+        begin_group(0, 0)
+        for t in range(4):
+            a = silu(first[t], 0, 0, t)
+            reduce(a, 0, 0, t)
+            if t:
+                scale(0, 0, t - 1)
+        scale(0, 0, 3)
+        un0 = group_add(0, 0)
+
+        begin_group(0, 1)
+        for t in range(4):
+            if t == 3:
+                group_quant(0, 0, group_permute(un0))
+            ps = bank(4 + t)
+            for g in range(8):
+                mm1(ps, 0, 1, t, g)
+            a = silu(ps, 0, 1, t)
+            reduce(a, 0, 1, t)
+            if t:
+                scale(0, 1, t - 1)
+        scale(0, 1, 3)
+        un1 = group_add(0, 1)
+
+        def stage1_b(k):
+            g2, t = divmod(k, 4)
+            if t == 0:
+                begin_group(1, g2)
+            ps = next_bank()
+            for g in range(8):
+                mm1(ps, 1, g2, t, g)
+            return ps
+
+        def post_a(k, ps):
+            g2, t = divmod(k, 4)
+            return silu(ps, 1, g2, t)
+
+        def post_b(k, a):
+            g2, t = divmod(k, 4)
+            reduce(a, 1, g2, t)
+
+        def post_c(k):
+            g2, t = divmod(k, 4)
+            scale(1, g2, t)
+
+        ps0 = stage1_b(0)
+        a0 = post_a(0, ps0)
+        pm = group_permute(un1)
+        ps1 = stage1_b(1)
+        group_quant(0, 1, pm)
+        post_b(0, a0)
+
+        items = [(h, n) for h in range(2) for n in range(8)]
+        zs = {0: zmm(0, 0)}
+        gts = {0: evac(zs[0], 0, 0)}
+        post_c(0)
+        a1 = post_a(1, ps1)
+        sts = {0: evac(zs[0], 0, 1)}
+        zs[1] = zmm(0, 1)
+        pend = None
+        un = None
+        pm = None
+        kprev = []
+        for i, (h, n) in enumerate(items):
+            gh = turn((gts[i], sts[i]), n)
+            k = i + 2
+            if k == 9:
+                zs[8] = zmm(*items[8])
+            if un is not None:
+                pm = group_permute(un)
+                un = None
+            for kp in kprev:
+                post_c(kp)
+                if kp == 3 or kp == 7:
+                    un = group_add(1, kp // 4)
+                    if kp == 7:
+                        pm = group_permute(un)
+                        un = None
+            kprev = [1] if i == 0 else []
+            more = i + 1 < 16
+            if more:
+                gts[i + 1] = evac(zs[i + 1], items[i + 1][1], 0)
+            gs = gate_copy(gh, h, n)
+            if more:
+                sts[i + 1] = evac(zs[i + 1], items[i + 1][1], 1)
+            if k < 8:
+                ps = stage1_b(k)
+            if k < 16 and k != 8:
+                zs[k] = zmm(*items[k])
+            o = product(gh, gs, h, n)
+            if i == 0:
+                post_b(1, a1)
+            if k < 8:
+                a = post_a(k, ps)
+            if pend:
+                add_store(*pend)
+            if k < 8:
+                post_b(k, a)
+                kprev.append(k)
+            if pm is not None:
+                group_quant(1, 0 if k < 8 else 1, pm)
+                pm = None
+            pend = (o, gh, h, n)
+        add_store(*pend, parts=2)

@@ -17,7 +17,8 @@ ACT = mybir.ActivationFunctionType
 ALU = mybir.AluOpType
 AX = mybir.AxisListType
 
-W_V = (384, 128, 128, 128, 128, 128, 192, 192, 176, 176, 176, 176, 176, 176, 176, 176)
+W_V = (384, 128, 128, 64, 64, 64, 160, 160, 176, 176, 176, 176, 176, 176, 176, 176)
+ST1_B = ((1,), (2,), (3, 4), (5,), (6,), (7,)) + ((),) * 10
 
 
 def tile_squeeze_excite_shift_f2_kernel(
@@ -34,9 +35,15 @@ def tile_squeeze_excite_shift_f2_kernel(
         def bank(i, shape=(128, 512), dtype=F32):
             return psum.tile(list(shape), dtype, name="bank%d" % i, tag="bank%d" % i)
 
-        xw = keep.tile([128, 8, 2048], U8, name="xw", align_bytes=64)
+        def big(shape, dtype, name):
+            return work.tile(shape, dtype, name=name, tag="big", bufs=8, align_bytes=64)
+
+        xw, w1 = [None, None], [None, None]
+        xw[0] = big([128, 8, 1024], U8, "xw0")
+        w1[0] = big([128, 8, 1024], U8, "w10")
+        w1[1] = big([128, 8, 1024], U8, "w11")
+        xw[1] = big([128, 8, 1024], U8, "xw1")
         xs = [keep.tile([128, 8, 512], U8, name="xs%d" % h, align_bytes=64) for h in range(2)]
-        w1 = keep.tile([128, 8, 2048], U8, name="w1", align_bytes=64)
         w1s = [keep.tile([128, 8, 512], U8, name="w1s%d" % g2, align_bytes=64) for g2 in range(2)]
         w2 = keep.tile([128, 2, 16384], U8, name="w2", align_bytes=64)
         w2s = keep.tile([128, 2, 8192], U8, name="w2s", align_bytes=64)
@@ -55,9 +62,9 @@ def tile_squeeze_excite_shift_f2_kernel(
         def zero(eng, t):
             eng.memset(t.rearrange("p g n -> p (g n)").bitcast(I32), 0)
 
-        nc.vector.memset(vr[64:128, :], 0.0)
         zero(nc.vector, xs[0][:])
         zero(nc.vector, w1s[0][:])
+        nc.vector.memset(vr[64:128, :], 0.0)
         zero(nc.vector, w1s[1][:])
         zero(nc.vector, xs[1][:])
         make_identity(nc, idb[:])
@@ -72,7 +79,7 @@ def tile_squeeze_excite_shift_f2_kernel(
 
         def load_words(dst, src, half, a, b):
             cols = slice(half * 1024, (half + 1) * 1024)
-            load(dst[:, a:b, cols].bitcast(I32), src[a:b, :, cols].rearrange("g p n -> p g n").bitcast(I32))
+            load(dst[half][:, a:b, :].bitcast(I32), src[a:b, :, cols].rearrange("g p n -> p g n").bitcast(I32))
 
         def load_scales(dst, src):
             for q in range(4):
@@ -114,12 +121,11 @@ def tile_squeeze_excite_shift_f2_kernel(
             load_y(1, q)
 
         def mm1(ps, h, g2, t, g):
-            col = g2 * 512 + t * 128
             nc.tensor.matmul_mx(
                 out=ps[:],
-                lhsT=w1[:, g, 2 * col:2 * col + 256].bitcast(FP4X4),
+                lhsT=w1[g2][:, g, t * 256:(t + 1) * 256].bitcast(FP4X4),
                 lhsT_scale=w1s[g2][:, g, t * 128:(t + 1) * 128],
-                rhs=xw[:, g, h * 1024:(h + 1) * 1024].bitcast(FP4X4),
+                rhs=xw[h][:, g, :].bitcast(FP4X4),
                 rhs_scale=xs[h][:, g, :],
                 start=(g == 0), stop=(g == 7))
 
@@ -149,7 +155,14 @@ def tile_squeeze_excite_shift_f2_kernel(
         def group_add(h, g2):
             asum, amax, usum, umax = acc[(h, g2)]
             un = work.tile([128, 4, 64], BF16, name="un", tag="un", align_bytes=64)
-            nc.vector.tensor_tensor(out=un[:], in0=usum[:], in1=umax[:], op=ALU.add)
+            for t in (2, 3):
+                r = 80 + 4 * g2 + t
+                nc.vector.tensor_scalar(out=umax[:, t, :], in0=amax[:, t, :], scalar1=cst[:, r:r + 1], scalar2=None, op0=ALU.mult)
+            nc.vector.tensor_tensor(out=un[:, 0:2, :], in0=usum[:, 0:2, :], in1=umax[:, 0:2, :], op=ALU.add)
+            for t in (2, 3):
+                r = 72 + 4 * g2 + t
+                nc.vector.scalar_tensor_tensor(out=un[:, t, :], in0=asum[:, t, :], scalar=cst[:, r:r + 1], in1=umax[:, t, :],
+                                               op0=ALU.mult, op1=ALU.add)
             return un
 
         ring = [0]
@@ -206,37 +219,34 @@ def tile_squeeze_excite_shift_f2_kernel(
                                          bias=cst[:, j:j + 1])
             return r
 
-        def turn(gs, n):
-            res = []
-            for part in range(2):
-                b = bank(4 + 2 * part + n % 2)
-                for ct in range(4):
-                    nc.tensor.transpose(b[:, ct * 128:(ct + 1) * 128], gs[part][:, ct, :], idf[:])
-                res.append(b)
-            return res
+        def turn(zt, n, part):
+            b = bank(4 + 2 * part + n % 2)
+            for ct in range(4):
+                nc.tensor.transpose(b[:, ct * 128:(ct + 1) * 128], zt[:, ct, :], idf[:])
+            return b
 
-        def gate_copy(gh, h, n):
+        def gate_copy(gate, h, n):
             w = W_V[8 * h + n]
             gs = work.tile([128, 512], F32, name="gs", tag="gs", bufs=3, align_bytes=64)
-            nc.scalar.activation(out=gs[:, w:512], in_=gh[0][:, w:512], func=ACT.Identity, bias=one[:])
+            nc.scalar.activation(out=gs[:, w:512], in_=gate[:, w:512], func=ACT.Identity, bias=one[:])
             return gs
 
-        def product(gh, gs, h, n):
-            o = work.tile([128, 4, 512], F32, name="o", tag="o", bufs=4, align_bytes=64)
+        def product(gate, gs, h, n):
+            o = big([128, 4, 512], F32, "o")
             w = W_V[8 * h + n]
             c0 = (n % 2) * 512
             yt = ys[h][n // 2]
             nc.gpsimd.tensor_tensor(out=o[:, :, w:512], in0=yt[:, :, c0 + w:c0 + 512],
                                     in1=gs[:, w:512].unsqueeze(1).to_broadcast([128, 4, 512 - w]), op=ALU.mult)
             nc.vector.scalar_tensor_tensor(
-                out=o[:, :, 0:w], in0=gh[0][:, 0:w].unsqueeze(1).to_broadcast([128, 4, w]), scalar=1.0,
+                out=o[:, :, 0:w], in0=gate[:, 0:w].unsqueeze(1).to_broadcast([128, 4, w]), scalar=1.0,
                 in1=yt[:, :, c0:c0 + w], op0=ALU.add, op1=ALU.mult)
             return o
 
-        def add_store(o, gh, h, n, parts=1):
+        def add_store(o, shift, h, n, parts=1):
             s = 4 // parts
             for j in range(0, 4, s):
-                sh = gh[1][:].unsqueeze(1).to_broadcast([128, s, 512])
+                sh = shift[:].unsqueeze(1).to_broadcast([128, s, 512])
                 nc.vector.scalar_tensor_tensor(out=o[:, j:j + s, :], in0=o[:, j:j + s, :], scalar=0.5, in1=sh,
                                                op0=ALU.mult, op1=ALU.add)
                 nc.sync.dma_start(out=rows(out, h)[:, j:j + s, n * 512:(n + 1) * 512], in_=o[:, j:j + s, :])
@@ -255,9 +265,8 @@ def tile_squeeze_excite_shift_f2_kernel(
         for t in range(4):
             a = silu(first[t], 0, 0, t)
             reduce(a, 0, 0, t)
-            if t:
+            if 0 < t < 3:
                 scale(0, 0, t - 1)
-        scale(0, 0, 3)
         un0 = group_add(0, 0)
 
         begin_group(0, 1)
@@ -269,9 +278,8 @@ def tile_squeeze_excite_shift_f2_kernel(
                 mm1(ps, 0, 1, t, g)
             a = silu(ps, 0, 1, t)
             reduce(a, 0, 1, t)
-            if t:
+            if 0 < t < 3:
                 scale(0, 1, t - 1)
-        scale(0, 1, 3)
         un1 = group_add(0, 1)
 
         def stage1_b(k):
@@ -298,59 +306,58 @@ def tile_squeeze_excite_shift_f2_kernel(
         ps0 = stage1_b(0)
         a0 = post_a(0, ps0)
         pm = group_permute(un1)
-        ps1 = stage1_b(1)
         group_quant(0, 1, pm)
         post_b(0, a0)
 
         items = [(h, n) for h in range(2) for n in range(8)]
         zs = {0: zmm(0, 0)}
         gts = {0: evac(zs[0], 0, 0)}
-        post_c(0)
-        a1 = post_a(1, ps1)
         sts = {0: evac(zs[0], 0, 1)}
         zs[1] = zmm(0, 1)
-        pend = None
+        post_c(0)
+        silus = []
+        sums = []
         un = None
         pm = None
-        kprev = []
         for i, (h, n) in enumerate(items):
-            gh = turn((gts[i], sts[i]), n)
-            k = i + 2
-            if k == 9:
+            if i:
+                shift = turn(sts[i - 1], items[i - 1][1], 1)
+            gate = turn(gts[i], n, 0)
+            if i == 7 and 8 not in zs:
                 zs[8] = zmm(*items[8])
             if un is not None:
-                pm = group_permute(un)
+                pm = (un[0], group_permute(un[1]))
                 un = None
-            for kp in kprev:
-                post_c(kp)
-                if kp == 3 or kp == 7:
-                    un = group_add(1, kp // 4)
-                    if kp == 7:
-                        pm = group_permute(un)
-                        un = None
-            kprev = [1] if i == 0 else []
             more = i + 1 < 16
             if more:
                 gts[i + 1] = evac(zs[i + 1], items[i + 1][1], 0)
-            gs = gate_copy(gh, h, n)
+            gs = gate_copy(gate, h, n)
             if more:
                 sts[i + 1] = evac(zs[i + 1], items[i + 1][1], 1)
-            if k < 8:
-                ps = stage1_b(k)
-            if k < 16 and k != 8:
-                zs[k] = zmm(*items[k])
-            o = product(gh, gs, h, n)
-            if i == 0:
-                post_b(1, a1)
-            if k < 8:
-                a = post_a(k, ps)
-            if pend:
-                add_store(*pend)
-            if k < 8:
-                post_b(k, a)
-                kprev.append(k)
-            if pm is not None:
-                group_quant(1, 0 if k < 8 else 1, pm)
+            new = [(j, stage1_b(j)) for j in ST1_B[i]]
+            if i + 2 < 16 and (i != 6 or (1, 1) in codes):
+                zs[i + 2] = zmm(*items[i + 2])
+            o = product(gate, gs, h, n)
+            for j, a in silus:
+                post_b(j, a)
+            for j in sums:
+                if j % 4 < 2:
+                    post_c(j)
+            for j, a in silus:
+                if j % 4 == 3:
+                    un = (j // 4, group_add(1, j // 4))
+                    if j == 7:
+                        pm = (1, group_permute(un[1]))
+                        un = None
+            sums = [j for j, a in silus]
+            silus = [(j, post_a(j, ps)) for j, ps in new]
+            if pm is not None and pm[0] == 1:
+                group_quant(1, 1, pm[1])
                 pm = None
-            pend = (o, gh, h, n)
-        add_store(*pend, parts=2)
+            if i:
+                add_store(pend, shift, *items[i - 1])
+            if pm is not None:
+                group_quant(1, pm[0], pm[1])
+                pm = None
+            pend = o
+        add_store(pend, turn(sts[15], 7, 1), 1, 7, parts=2)

@@ -53,7 +53,7 @@ def tile_squeeze_excite_shift_f2_kernel(
         sel = keep.tile([128, 4, 224], BF16, name="sel", align_bytes=64)
         vr = keep.tile([128, 128], BF16, name="vr", align_bytes=64)
         cst = keep.tile([128, 88], F32, name="cst", align_bytes=64)
-        one = keep.tile([128, 1], F32, name="one")
+        half = keep.tile([128, 1], F32, name="half")
         dummy = keep.tile([128, 1], F32, name="dummy")
 
         nc.gpsimd.memset(dummy[:], 0.0)
@@ -69,7 +69,7 @@ def tile_squeeze_excite_shift_f2_kernel(
         zero(nc.vector, xs[1][:])
         make_identity(nc, idb[:])
         zero(nc.gpsimd, w2s[:])
-        nc.gpsimd.memset(one[:], 1.0)
+        nc.gpsimd.memset(half[:], 0.5)
         make_identity(nc, idf[:])
         nc.vector.memset(sel[:], 0.0)
         nc.vector.tensor_copy(out=sel[:, :, 96:128], in_=idb[:].rearrange("p (i t) -> p t i", t=4))
@@ -225,31 +225,31 @@ def tile_squeeze_excite_shift_f2_kernel(
                 nc.tensor.transpose(b[:, ct * 128:(ct + 1) * 128], zt[:, ct, :], idf[:])
             return b
 
-        def gate_copy(gate, h, n):
-            w = W_V[8 * h + n]
-            gs = work.tile([128, 512], F32, name="gs", tag="gs", bufs=3, align_bytes=64)
-            nc.scalar.activation(out=gs[:, w:512], in_=gate[:, w:512], func=ACT.Identity, bias=one[:])
-            return gs
+        def halve(gt):
+            flat = gt[:].rearrange("p t i -> p (t i)")
+            nc.scalar.activation(out=flat, in_=flat, func=ACT.Identity, bias=half[:], scale=0.5)
 
-        def product(gate, gs, h, n):
+        def product(gate, h, n):
             o = big([128, 4, 512], F32, "o")
-            w = W_V[8 * h + n]
             c0 = (n % 2) * 512
-            yt = ys[h][n // 2]
-            nc.gpsimd.tensor_tensor(out=o[:, :, w:512], in0=yt[:, :, c0 + w:c0 + 512],
-                                    in1=gs[:, w:512].unsqueeze(1).to_broadcast([128, 4, 512 - w]), op=ALU.mult)
-            nc.vector.scalar_tensor_tensor(
-                out=o[:, :, 0:w], in0=gate[:, 0:w].unsqueeze(1).to_broadcast([128, 4, w]), scalar=1.0,
-                in1=yt[:, :, c0:c0 + w], op0=ALU.add, op1=ALU.mult)
+            nc.vector.tensor_tensor(out=o[:], in0=gate[:].unsqueeze(1).to_broadcast([128, 4, 512]),
+                                    in1=ys[h][n // 2][:, :, c0:c0 + 512], op=ALU.mult)
             return o
 
-        def add_store(o, shift, h, n, parts=1):
-            s = 4 // parts
-            for j in range(0, 4, s):
-                sh = shift[:].unsqueeze(1).to_broadcast([128, s, 512])
-                nc.vector.scalar_tensor_tensor(out=o[:, j:j + s, :], in0=o[:, j:j + s, :], scalar=0.5, in1=sh,
-                                               op0=ALU.mult, op1=ALU.add)
-                nc.sync.dma_start(out=rows(out, h)[:, j:j + s, n * 512:(n + 1) * 512], in_=o[:, j:j + s, :])
+        def shift_copy(shift, i):
+            w = W_V[i]
+            ss = work.tile([128, 512], F32, name="ss", tag="ss", bufs=3, align_bytes=64)
+            nc.scalar.activation(out=ss[:, w:512], in_=shift[:, w:512], func=ACT.Copy)
+            return ss
+
+        def add_store(o, shift, ss, i):
+            h, n = divmod(i, 8)
+            w = W_V[i]
+            nc.gpsimd.tensor_tensor(out=o[:, :, w:512], in0=o[:, :, w:512],
+                                    in1=ss[:, w:512].unsqueeze(1).to_broadcast([128, 4, 512 - w]), op=ALU.add)
+            nc.vector.tensor_tensor(out=o[:, :, 0:w], in0=o[:, :, 0:w],
+                                    in1=shift[:, 0:w].unsqueeze(1).to_broadcast([128, 4, w]), op=ALU.add)
+            nc.sync.dma_start(out=rows(out, h)[:, :, n * 512:(n + 1) * 512], in_=o[:])
 
         first = [bank(t) for t in range(4)]
         for g in range(8):
@@ -312,6 +312,7 @@ def tile_squeeze_excite_shift_f2_kernel(
         items = [(h, n) for h in range(2) for n in range(8)]
         zs = {0: zmm(0, 0)}
         gts = {0: evac(zs[0], 0, 0)}
+        halve(gts[0])
         sts = {0: evac(zs[0], 0, 1)}
         zs[1] = zmm(0, 1)
         post_c(0)
@@ -328,16 +329,16 @@ def tile_squeeze_excite_shift_f2_kernel(
             if un is not None:
                 pm = (un[0], group_permute(un[1]))
                 un = None
-            more = i + 1 < 16
-            if more:
+            if i:
+                ss = shift_copy(shift, i - 1)
+            if i + 1 < 16:
                 gts[i + 1] = evac(zs[i + 1], items[i + 1][1], 0)
-            gs = gate_copy(gate, h, n)
-            if more:
+                halve(gts[i + 1])
                 sts[i + 1] = evac(zs[i + 1], items[i + 1][1], 1)
             new = [(j, stage1_b(j)) for j in ST1_B[i]]
             if i + 2 < 16 and (i != 6 or (1, 1) in codes):
                 zs[i + 2] = zmm(*items[i + 2])
-            o = product(gate, gs, h, n)
+            o = product(gate, h, n)
             for j, a in silus:
                 post_b(j, a)
             for j in sums:
@@ -355,9 +356,10 @@ def tile_squeeze_excite_shift_f2_kernel(
                 group_quant(1, 1, pm[1])
                 pm = None
             if i:
-                add_store(pend, shift, *items[i - 1])
+                add_store(pend, shift, ss, i - 1)
             if pm is not None:
                 group_quant(1, pm[0], pm[1])
                 pm = None
             pend = o
-        add_store(pend, turn(sts[15], 7, 1), 1, 7, parts=2)
+        shift = turn(sts[15], 7, 1)
+        add_store(pend, shift, shift_copy(shift, 15), 15)

@@ -17,7 +17,7 @@ ACT = mybir.ActivationFunctionType
 ALU = mybir.AluOpType
 AX = mybir.AxisListType
 
-W_V = (384, 128, 128, 64, 64, 64, 160, 160, 176, 176, 176, 176, 176, 176, 176, 176)
+J_V = 2
 ST1_B = ((1,), (2,), (3, 4), (5,), (6,), (7,)) + ((),) * 10
 
 
@@ -132,7 +132,8 @@ def tile_squeeze_excite_shift_f2_kernel(
         acc = {}
 
         def begin_group(h, g2):
-            acc[(h, g2)] = [work.tile([128, 4, 64], F32, name=s, tag=s) for s in ("asum", "amax", "usum", "umax")]
+            acc[(h, g2)] = [work.tile([128, 4, 64], F32, name=s, tag=s) for s in ("asum", "amax")] + [
+                work.tile([128, 4, 64], BF16, name="un", tag="un", bufs=3, align_bytes=64)]
 
         def silu(ps, h, g2, t):
             a = work.tile([128, 512], F32, name="a", tag="a", bufs=4)
@@ -141,29 +142,25 @@ def tile_squeeze_excite_shift_f2_kernel(
             return a
 
         def reduce(a, h, g2, t):
-            asum, amax, usum, umax = acc[(h, g2)]
+            asum, amax, un = acc[(h, g2)]
             av = a[:].rearrange("p (i j) -> p i j", j=8)
-            nc.vector.tensor_reduce(out=asum[:, t, :], in_=av, axis=AX.X, op=ALU.add)
             nc.vector.tensor_reduce(out=amax[:, t, :], in_=av, axis=AX.X, op=ALU.max)
+            if (h, g2) == (0, 0):
+                s4 = work.tile([128, 64, 4], F32, name="s4", tag="s4")
+                s2 = work.tile([128, 64, 2], F32, name="s2", tag="s2")
+                nc.gpsimd.tensor_tensor(out=s4[:], in0=av[:, :, 0:4], in1=av[:, :, 4:8], op=ALU.add)
+                nc.gpsimd.tensor_tensor(out=s2[:], in0=s4[:, :, 0:2], in1=s4[:, :, 2:4], op=ALU.add)
+                nc.gpsimd.tensor_tensor(out=asum[:, t, :], in0=s2[:, :, 0], in1=s2[:, :, 1], op=ALU.add)
+            else:
+                nc.vector.tensor_reduce(out=asum[:, t, :], in_=av, axis=AX.X, op=ALU.add)
+            r = 80 + 4 * g2 + t
+            nc.vector.tensor_scalar(out=amax[:, t, :], in0=amax[:, t, :], scalar1=cst[:, r:r + 1], scalar2=None, op0=ALU.mult)
 
-        def scale(h, g2, t):
-            asum, amax, usum, umax = acc[(h, g2)]
-            for src, dst, r in ((asum, usum, 72), (amax, umax, 80)):
-                r = r + 4 * g2 + t
-                nc.scalar.activation(out=dst[:, t, :], in_=src[:, t, :], func=ACT.Copy, scale=cst[:, r:r + 1])
-
-        def group_add(h, g2):
-            asum, amax, usum, umax = acc[(h, g2)]
-            un = work.tile([128, 4, 64], BF16, name="un", tag="un", align_bytes=64)
-            for t in (2, 3):
-                r = 80 + 4 * g2 + t
-                nc.vector.tensor_scalar(out=umax[:, t, :], in0=amax[:, t, :], scalar1=cst[:, r:r + 1], scalar2=None, op0=ALU.mult)
-            nc.vector.tensor_tensor(out=un[:, 0:2, :], in0=usum[:, 0:2, :], in1=umax[:, 0:2, :], op=ALU.add)
-            for t in (2, 3):
-                r = 72 + 4 * g2 + t
-                nc.vector.scalar_tensor_tensor(out=un[:, t, :], in0=asum[:, t, :], scalar=cst[:, r:r + 1], in1=umax[:, t, :],
-                                               op0=ALU.mult, op1=ALU.add)
-            return un
+        def mix(h, g2, t):
+            asum, amax, un = acc[(h, g2)]
+            r = 72 + 4 * g2 + t
+            nc.vector.scalar_tensor_tensor(out=un[:, t, :], in0=asum[:, t, :], scalar=cst[:, r:r + 1], in1=amax[:, t, :],
+                                           op0=ALU.mult, op1=ALU.add)
 
         ring = [0]
 
@@ -171,7 +168,8 @@ def tile_squeeze_excite_shift_f2_kernel(
             ring[0] += 1
             return bank((ring[0] - 1) % 4, shape)
 
-        def group_permute(un):
+        def group_permute(h, g2):
+            un = acc[(h, g2)][2]
             ps = next_bank((128, 4, 64))
             for t in range(4):
                 for s in range(4):
@@ -232,24 +230,28 @@ def tile_squeeze_excite_shift_f2_kernel(
         def product(gate, h, n):
             o = big([128, 4, 512], F32, "o")
             c0 = (n % 2) * 512
-            nc.vector.tensor_tensor(out=o[:], in0=gate[:].unsqueeze(1).to_broadcast([128, 4, 512]),
-                                    in1=ys[h][n // 2][:, :, c0:c0 + 512], op=ALU.mult)
+            nc.vector.tensor_tensor(out=o[:], in0=ys[h][n // 2][:, :, c0:c0 + 512],
+                                    in1=gate[:].unsqueeze(1).to_broadcast([128, 4, 512]), op=ALU.mult)
             return o
 
         def shift_copy(shift, i):
-            w = W_V[i]
             ss = work.tile([128, 512], F32, name="ss", tag="ss", bufs=3, align_bytes=64)
-            nc.scalar.activation(out=ss[:, w:512], in_=shift[:, w:512], func=ACT.Copy)
+            nc.scalar.activation(out=ss[:], in_=shift[:], func=ACT.Copy)
             return ss
 
-        def add_store(o, shift, ss, i):
+        def store(o, i, a, b):
             h, n = divmod(i, 8)
-            w = W_V[i]
-            nc.gpsimd.tensor_tensor(out=o[:, :, w:512], in0=o[:, :, w:512],
-                                    in1=ss[:, w:512].unsqueeze(1).to_broadcast([128, 4, 512 - w]), op=ALU.add)
-            nc.vector.tensor_tensor(out=o[:, :, 0:w], in0=o[:, :, 0:w],
-                                    in1=shift[:, 0:w].unsqueeze(1).to_broadcast([128, 4, w]), op=ALU.add)
-            nc.sync.dma_start(out=rows(out, h)[:, :, n * 512:(n + 1) * 512], in_=o[:])
+            nc.sync.dma_start(out=rows(out, h)[:, a:b, n * 512:(n + 1) * 512], in_=o[:, a:b, :])
+
+        def add_v(o, shift, i, a, b):
+            nc.vector.tensor_tensor(out=o[:, a:b, :], in0=o[:, a:b, :],
+                                    in1=shift[:].unsqueeze(1).to_broadcast([128, b - a, 512]), op=ALU.add)
+            store(o, i, a, b)
+
+        def add_g(o, ss, i, a, b):
+            for j in range(a, b):
+                nc.gpsimd.tensor_tensor(out=o[:, j, :], in0=o[:, j, :], in1=ss[:], op=ALU.add)
+            store(o, i, a, b)
 
         first = [bank(t) for t in range(4)]
         for g in range(8):
@@ -263,24 +265,21 @@ def tile_squeeze_excite_shift_f2_kernel(
                 nc.vector.tensor_scalar(out=cst[:, 72:80], in0=cst[:, 72:80], scalar1=0.125, scalar2=None, op0=ALU.mult)
         begin_group(0, 0)
         for t in range(4):
-            a = silu(first[t], 0, 0, t)
-            reduce(a, 0, 0, t)
-            if 0 < t < 3:
-                scale(0, 0, t - 1)
-        un0 = group_add(0, 0)
+            reduce(silu(first[t], 0, 0, t), 0, 0, t)
 
         begin_group(0, 1)
         for t in range(4):
-            if t == 3:
-                group_quant(0, 0, group_permute(un0))
             ps = bank(4 + t)
             for g in range(8):
                 mm1(ps, 0, 1, t, g)
             a = silu(ps, 0, 1, t)
             reduce(a, 0, 1, t)
-            if 0 < t < 3:
-                scale(0, 1, t - 1)
-        un1 = group_add(0, 1)
+            if t:
+                mix(0, 1, t - 1)
+            if t == 2:
+                for s in range(4):
+                    mix(0, 0, s)
+        mix(0, 1, 3)
 
         def stage1_b(k):
             g2, t = divmod(k, 4)
@@ -291,23 +290,17 @@ def tile_squeeze_excite_shift_f2_kernel(
                 mm1(ps, 1, g2, t, g)
             return ps
 
-        def post_a(k, ps):
-            g2, t = divmod(k, 4)
-            return silu(ps, 1, g2, t)
-
-        def post_b(k, a):
-            g2, t = divmod(k, 4)
-            reduce(a, 1, g2, t)
-
-        def post_c(k):
-            g2, t = divmod(k, 4)
-            scale(1, g2, t)
+        def post(k, ps):
+            return silu(ps, 1, *divmod(k, 4))
 
         ps0 = stage1_b(0)
-        a0 = post_a(0, ps0)
-        pm = group_permute(un1)
-        group_quant(0, 1, pm)
-        post_b(0, a0)
+        a0 = post(0, ps0)
+        pm = group_permute(0, 0)
+        pm2 = group_permute(0, 1)
+        group_quant(0, 0, pm)
+        group_quant(0, 1, pm2)
+        reduce(a0, 1, 0, 0)
+        mix(1, 0, 0)
 
         items = [(h, n) for h in range(2) for n in range(8)]
         zs = {0: zmm(0, 0)}
@@ -315,20 +308,16 @@ def tile_squeeze_excite_shift_f2_kernel(
         halve(gts[0])
         sts = {0: evac(zs[0], 0, 1)}
         zs[1] = zmm(0, 1)
-        post_c(0)
         silus = []
-        sums = []
-        un = None
-        pm = None
+        ready = None
         for i, (h, n) in enumerate(items):
             if i:
                 shift = turn(sts[i - 1], items[i - 1][1], 1)
             gate = turn(gts[i], n, 0)
+            if ready is not None and ready == 0:
+                pm = group_permute(1, 0)
             if i == 7 and 8 not in zs:
                 zs[8] = zmm(*items[8])
-            if un is not None:
-                pm = (un[0], group_permute(un[1]))
-                un = None
             if i:
                 ss = shift_copy(shift, i - 1)
             if i + 1 < 16:
@@ -340,26 +329,26 @@ def tile_squeeze_excite_shift_f2_kernel(
                 zs[i + 2] = zmm(*items[i + 2])
             o = product(gate, h, n)
             for j, a in silus:
-                post_b(j, a)
-            for j in sums:
-                if j % 4 < 2:
-                    post_c(j)
-            for j, a in silus:
-                if j % 4 == 3:
-                    un = (j // 4, group_add(1, j // 4))
-                    if j == 7:
-                        pm = (1, group_permute(un[1]))
-                        un = None
-            sums = [j for j, a in silus]
-            silus = [(j, post_a(j, ps)) for j, ps in new]
-            if pm is not None and pm[0] == 1:
-                group_quant(1, 1, pm[1])
-                pm = None
+                reduce(a, 1, *divmod(j, 4))
+            last = silus and silus[-1][0] == 7
+            if last:
+                mix(1, 1, 3)
+                pm = group_permute(1, 1)
             if i:
-                add_store(pend, shift, ss, i - 1)
-            if pm is not None:
-                group_quant(1, pm[0], pm[1])
-                pm = None
+                add_v(pend, shift, i - 1, 0, J_V)
+                add_g(pend, ss, i - 1, J_V, 4)
+            if last:
+                group_quant(1, 1, pm)
+            for j, a in silus:
+                if j != 7:
+                    mix(1, *divmod(j, 4))
+            if ready == 0:
+                group_quant(1, 0, pm)
+                ready = None
+            if silus and silus[-1][0] in (3, 4) and (1, 0) not in codes:
+                ready = 0
+            silus = [(j, post(j, ps)) for j, ps in new]
             pend = o
         shift = turn(sts[15], 7, 1)
-        add_store(pend, shift, shift_copy(shift, 15), 15)
+        add_v(pend, shift, 15, 0, 2)
+        add_v(pend, shift, 15, 2, 4)

@@ -17,8 +17,8 @@ ACT = mybir.ActivationFunctionType
 ALU = mybir.AluOpType
 AX = mybir.AxisListType
 
-J_V = 2
-ST1_B = ((1,), (2,), (3, 4), (5,), (6,), (7,)) + ((),) * 10
+J_V = (1,) * 6 + (2, 2) + (2, 1) * 4
+ST1_B = ((1,), (2,), (3, 4), (5, 6), (7,)) + ((),) * 11
 
 
 def tile_squeeze_excite_shift_f2_kernel(
@@ -36,18 +36,17 @@ def tile_squeeze_excite_shift_f2_kernel(
             return psum.tile(list(shape), dtype, name="bank%d" % i, tag="bank%d" % i)
 
         def big(shape, dtype, name):
-            return work.tile(shape, dtype, name=name, tag="big", bufs=8, align_bytes=64)
+            return work.tile(shape, dtype, name=name, tag="big", bufs=4, align_bytes=64)
 
-        xw, w1 = [None, None], [None, None]
-        xw[0] = big([128, 8, 1024], U8, "xw0")
-        w1[0] = big([128, 8, 1024], U8, "w10")
-        w1[1] = big([128, 8, 1024], U8, "w11")
-        xw[1] = big([128, 8, 1024], U8, "xw1")
+        early = big([128, 2, 8, 1024], U8, "early")
+        late = big([128, 2, 8, 1024], U8, "late")
+        xw = [early[:, 0], late[:, 0]]
+        w1 = [early[:, 1], late[:, 1]]
         xs = [keep.tile([128, 8, 512], U8, name="xs%d" % h, align_bytes=64) for h in range(2)]
         w1s = [keep.tile([128, 8, 512], U8, name="w1s%d" % g2, align_bytes=64) for g2 in range(2)]
         w2 = keep.tile([128, 2, 16384], U8, name="w2", align_bytes=64)
         w2s = keep.tile([128, 2, 8192], U8, name="w2s", align_bytes=64)
-        ys = [[keep.tile([128, 4, 1024], BF16, name="y%d_%d" % (h, q), align_bytes=64) for q in range(4)] for h in range(2)]
+        ys = [[keep.tile([128, 4, 2048], BF16, name="y%d_%d" % (h, q), align_bytes=64) for q in range(2)] for h in range(2)]
         idf = keep.tile([128, 128], F32, name="idf", align_bytes=64)
         idb = keep.tile([128, 128], BF16, name="idb", align_bytes=64)
         sel = keep.tile([128, 4, 224], BF16, name="sel", align_bytes=64)
@@ -63,14 +62,14 @@ def tile_squeeze_excite_shift_f2_kernel(
             eng.memset(t.rearrange("p g n -> p (g n)").bitcast(I32), 0)
 
         zero(nc.vector, xs[0][:])
-        zero(nc.vector, w1s[0][:])
+        zero(nc.gpsimd, w1s[0][:])
         nc.vector.memset(vr[64:128, :], 0.0)
         zero(nc.vector, w1s[1][:])
         zero(nc.vector, xs[1][:])
         make_identity(nc, idb[:])
-        zero(nc.gpsimd, w2s[:])
         nc.gpsimd.memset(half[:], 0.5)
         make_identity(nc, idf[:])
+        zero(nc.gpsimd, w2s[:])
         nc.vector.memset(sel[:], 0.0)
         nc.vector.tensor_copy(out=sel[:, :, 96:128], in_=idb[:].rearrange("p (i t) -> p t i", t=4))
 
@@ -81,21 +80,22 @@ def tile_squeeze_excite_shift_f2_kernel(
             cols = slice(half * 1024, (half + 1) * 1024)
             load(dst[half][:, a:b, :].bitcast(I32), src[a:b, :, cols].rearrange("g p n -> p g n").bitcast(I32))
 
-        def load_scales(dst, src):
-            for q in range(4):
-                load(dst[32 * q:32 * q + 4, :, :].bitcast(I32),
-                     src[:, 4 * q:4 * q + 4, :].rearrange("g r n -> r g n").bitcast(I32))
+        def load_scales(dst, src, queue=nc.sync):
+            for r in range(4):
+                queue.dma_start(out=dst[r:128:32, :, :].bitcast(I32),
+                                in_=src[:, r:16:4, :].rearrange("g q n -> q g n").bitcast(I32))
 
-        def load_w2(part, q):
-            c0 = part * 8192 + q * 2048
-            load(w2[:, :, c0:c0 + 2048].bitcast(I32),
-                 w2_words[:, :, c0:c0 + 2048].rearrange("g p n -> p g n").bitcast(I32))
+        def load_w2(a, b):
+            for part in range(2):
+                c0, c1 = part * 8192 + 2 * a, part * 8192 + 2 * b
+                load(w2[:, :, c0:c1].bitcast(I32), w2_words[:, :, c0:c1].rearrange("g p n -> p g n").bitcast(I32))
 
         def rows(t, h):
             return t[64 * h:64 * h + 64].rearrange("i (r j) c -> (i r) j c", r=2)
 
-        def load_y(h, q):
-            load(ys[h][q][:], rows(y, h)[:, :, q * 1024:(q + 1) * 1024])
+        def load_y(h, a, b):
+            q = a // 2048
+            load(ys[h][q][:, :, a - 2048 * q:b - 2048 * q], rows(y, h)[:, :, a:b])
 
         load_words(xw, x_words, 0, 0, 2)
         load_words(w1, w1_words, 0, 0, 2)
@@ -112,13 +112,12 @@ def tile_squeeze_excite_shift_f2_kernel(
         load_scales(w1s[1], w1_scales[:, :, 512:1024])
         load_words(xw, x_words, 1, 0, 8)
         load_scales(xs[1], x_scales[:, :, 512:1024])
-        load_scales(w2s, w2_scales)
-        for q in range(4):
-            load_w2(0, q)
-            load_w2(1, q)
-            load_y(0, q)
-        for q in range(4):
-            load_y(1, q)
+        load_scales(w2s, w2_scales, nc.gpsimd)
+        for a, b in ((0, 1024), (1024, 2048), (2048, 4096)):
+            load_w2(a, b)
+            load_y(0, a, b)
+        for a in (0, 2048):
+            load_y(1, a, a + 2048)
 
         def mm1(ps, h, g2, t, g):
             nc.tensor.matmul_mx(
@@ -227,31 +226,37 @@ def tile_squeeze_excite_shift_f2_kernel(
             flat = gt[:].rearrange("p t i -> p (t i)")
             nc.scalar.activation(out=flat, in_=flat, func=ACT.Identity, bias=half[:], scale=0.5)
 
-        def product(gate, h, n):
-            o = big([128, 4, 512], F32, "o")
-            c0 = (n % 2) * 512
-            nc.vector.tensor_tensor(out=o[:], in0=ys[h][n // 2][:, :, c0:c0 + 512],
+        def product(o, gate, h, n):
+            c0 = (n % 4) * 512
+            nc.vector.tensor_tensor(out=o, in0=ys[h][n // 4][:, :, c0:c0 + 512],
                                     in1=gate[:].unsqueeze(1).to_broadcast([128, 4, 512]), op=ALU.mult)
-            return o
 
         def shift_copy(shift, i):
             ss = work.tile([128, 512], F32, name="ss", tag="ss", bufs=3, align_bytes=64)
             nc.scalar.activation(out=ss[:], in_=shift[:], func=ACT.Copy)
             return ss
 
-        def store(o, i, a, b):
-            h, n = divmod(i, 8)
-            nc.sync.dma_start(out=rows(out, h)[:, a:b, n * 512:(n + 1) * 512], in_=o[:, a:b, :])
+        def store(src, i, a, b, c0, c1):
+            h = i // 8
+            nc.sync.dma_start(out=rows(out, h)[:, a:b, c0:c1], in_=src)
 
-        def add_v(o, shift, i, a, b):
+        def add_v(o, shift, a, b):
             nc.vector.tensor_tensor(out=o[:, a:b, :], in0=o[:, a:b, :],
                                     in1=shift[:].unsqueeze(1).to_broadcast([128, b - a, 512]), op=ALU.add)
-            store(o, i, a, b)
 
-        def add_g(o, ss, i, a, b):
+        def add_g(o, ss, a, b):
             for j in range(a, b):
                 nc.gpsimd.tensor_tensor(out=o[:, j, :], in0=o[:, j, :], in1=ss[:], op=ALU.add)
-            store(o, i, a, b)
+
+        def finish_chunk(pair, o, shift, ss, i):
+            c0 = (i % 8) * 512
+            add_v(o, shift, 0, J_V[i])
+            add_g(o, ss, J_V[i], 4)
+            for j in (0, 2):
+                if i == 14:
+                    store(o[:, j:j + 2, :], i, j, j + 2, c0, c0 + 512)
+                elif i % 2:
+                    store(pair[:, j:j + 2, :], i, j, j + 2, c0 - 512, c0 + 512)
 
         first = [bank(t) for t in range(4)]
         for g in range(8):
@@ -314,20 +319,23 @@ def tile_squeeze_excite_shift_f2_kernel(
             if i:
                 shift = turn(sts[i - 1], items[i - 1][1], 1)
             gate = turn(gts[i], n, 0)
-            if ready is not None and ready == 0:
-                pm = group_permute(1, 0)
             if i == 7 and 8 not in zs:
                 zs[8] = zmm(*items[8])
             if i:
                 ss = shift_copy(shift, i - 1)
             if i + 1 < 16:
                 gts[i + 1] = evac(zs[i + 1], items[i + 1][1], 0)
-                halve(gts[i + 1])
                 sts[i + 1] = evac(zs[i + 1], items[i + 1][1], 1)
+                halve(gts[i + 1])
             new = [(j, stage1_b(j)) for j in ST1_B[i]]
+            if ready == 0:
+                pm = group_permute(1, 0)
             if i + 2 < 16 and (i != 6 or (1, 1) in codes):
                 zs[i + 2] = zmm(*items[i + 2])
-            o = product(gate, h, n)
+            if i % 2 == 0:
+                pair = big([128, 4, 1024], F32, "pair")
+            o = pair[:, :, (i % 2) * 512:(i % 2) * 512 + 512]
+            product(o, gate, h, n)
             for j, a in silus:
                 reduce(a, 1, *divmod(j, 4))
             last = silus and silus[-1][0] == 7
@@ -335,8 +343,7 @@ def tile_squeeze_excite_shift_f2_kernel(
                 mix(1, 1, 3)
                 pm = group_permute(1, 1)
             if i:
-                add_v(pend, shift, i - 1, 0, J_V)
-                add_g(pend, ss, i - 1, J_V, 4)
+                finish_chunk(*pend, shift, ss, i - 1)
             if last:
                 group_quant(1, 1, pm)
             for j, a in silus:
@@ -348,7 +355,8 @@ def tile_squeeze_excite_shift_f2_kernel(
             if silus and silus[-1][0] in (3, 4) and (1, 0) not in codes:
                 ready = 0
             silus = [(j, post(j, ps)) for j, ps in new]
-            pend = o
+            pend = (pair, o)
         shift = turn(sts[15], 7, 1)
-        add_v(pend, shift, 15, 0, 2)
-        add_v(pend, shift, 15, 2, 4)
+        for a, b in ((0, 2), (2, 3), (3, 4)):
+            add_v(o, shift, a, b)
+            store(o[:, a:b, :], 15, a, b, 3584, 4096)

from contextlib import ExitStack

import concourse.mybir as mybir
from concourse.masks import make_identity

B, P, M, C, R, E = 128, 8, 1024, 4096, 1024, 8192
FLOPS = 2 * M * C * R + 2 * B * R * E

F32 = mybir.dt.float32
BF16 = mybir.dt.bfloat16
U32 = mybir.dt.uint32
I32 = mybir.dt.int32
U8 = mybir.dt.uint8
FP8X4 = mybir.dt.float8_e4m3fn_x4
FP4X4 = mybir.dt.float4_e2m1fn_x4
ACT = mybir.ActivationFunctionType
ALU = mybir.AluOpType
AX = mybir.AxisListType

J_V = (1,) * 6 + (2, 2) + (2, 1) * 4
ST1_B = ((1,), (2,), (3, 4), (5, 6), (7,)) + ((),) * 11


def tile_squeeze_excite_shift_f2_kernel(
    tc, x_words, x_scales, w1_words, w1_scales, b1, gain_mean, gain_max,
    w2_words, w2_scales, b2, y, out,
):
    nc = tc.nc
    with ExitStack() as ctx:
        keep = ctx.enter_context(tc.tile_pool(name="keep", bufs=1))
        work = ctx.enter_context(tc.tile_pool(name="work", bufs=2))
        psum = ctx.enter_context(tc.psum_pool(name="psum", bufs=1))
        ctx.enter_context(tc.manual_schedule())

        def bank(i, shape=(128, 512), dtype=F32):
            return psum.tile(list(shape), dtype, name="bank%d" % i, tag="bank%d" % i)

        def big(shape, dtype, name):
            return work.tile(shape, dtype, name=name, tag="big", bufs=4, align_bytes=64)

        early = big([128, 2, 8, 1024], U8, "early")
        late = big([128, 2, 8, 1024], U8, "late")
        xw = [early[:, 0], late[:, 0]]
        w1 = [early[:, 1], late[:, 1]]
        xs = [keep.tile([128, 8, 512], U8, name="xs%d" % h, align_bytes=64) for h in range(2)]
        w1s = [keep.tile([128, 8, 512], U8, name="w1s%d" % g2, align_bytes=64) for g2 in range(2)]
        w2 = keep.tile([128, 2, 16384], U8, name="w2", align_bytes=64)
        w2s = keep.tile([128, 2, 8192], U8, name="w2s", align_bytes=64)
        ys = [[keep.tile([128, 4, 2048], BF16, name="y%d_%d" % (h, q), align_bytes=64) for q in range(2)] for h in range(2)]
        idf = keep.tile([128, 128], F32, name="idf", align_bytes=64)
        idb = keep.tile([128, 128], BF16, name="idb", align_bytes=64)
        sel = keep.tile([128, 4, 224], BF16, name="sel", align_bytes=64)
        vr = keep.tile([128, 128], BF16, name="vr", align_bytes=64)
        cst = keep.tile([128, 88], F32, name="cst", align_bytes=64)
        half = keep.tile([128, 1], F32, name="half")
        dummy = keep.tile([128, 1], F32, name="dummy")

        nc.gpsimd.memset(dummy[:], 0.0)
        nc.scalar.activation(out=dummy[:], in_=dummy[:], func=ACT.Silu)

        def zero(eng, t):
            eng.memset(t.rearrange("p g n -> p (g n)").bitcast(I32), 0)

        zero(nc.vector, xs[0][:])
        zero(nc.gpsimd, w1s[0][:])
        nc.vector.memset(vr[64:128, :], 0.0)
        zero(nc.vector, w1s[1][:])
        zero(nc.vector, xs[1][:])
        make_identity(nc, idb[:])
        nc.gpsimd.memset(half[:], 0.5)
        make_identity(nc, idf[:])
        zero(nc.gpsimd, w2s[:])
        nc.vector.memset(sel[:], 0.0)
        nc.vector.tensor_copy(out=sel[:, :, 96:128], in_=idb[:].rearrange("p (i t) -> p t i", t=4))

        def load(dst, src):
            nc.sync.dma_start(out=dst, in_=src)

        def load_words(dst, src, half, a, b):
            cols = slice(half * 1024, (half + 1) * 1024)
            load(dst[half][:, a:b, :].bitcast(I32), src[a:b, :, cols].rearrange("g p n -> p g n").bitcast(I32))

        def load_scales(dst, src, queue=nc.sync):
            for r in range(4):
                queue.dma_start(out=dst[r:128:32, :, :].bitcast(I32),
                                in_=src[:, r:16:4, :].rearrange("g q n -> q g n").bitcast(I32))

        def load_w2(a, b):
            for part in range(2):
                c0, c1 = part * 8192 + 2 * a, part * 8192 + 2 * b
                load(w2[:, :, c0:c1].bitcast(I32), w2_words[:, :, c0:c1].rearrange("g p n -> p g n").bitcast(I32))

        def rows(t, h):
            return t[64 * h:64 * h + 64].rearrange("i (r j) c -> (i r) j c", r=2)

        def load_y(h, a, b):
            q = a // 2048
            load(ys[h][q][:, :, a - 2048 * q:b - 2048 * q], rows(y, h)[:, :, a:b])

        load_words(xw, x_words, 0, 0, 2)
        load_words(w1, w1_words, 0, 0, 2)
        load_scales(xs[0], x_scales[:, :, 0:512])
        load_scales(w1s[0], w1_scales[:, :, 0:512])
        load_words(w1, w1_words, 0, 2, 5)
        load_words(xw, x_words, 0, 2, 5)
        load_words(w1, w1_words, 0, 5, 8)
        load_words(xw, x_words, 0, 5, 8)
        load(vr[0:64, :], b2.rearrange("(t p) -> t p", p=128))
        for i, v in enumerate((b1, gain_mean, gain_max)):
            load(vr[64 + 8 * i:72 + 8 * i, :], v.rearrange("(t p) -> t p", p=128))
        load_words(w1, w1_words, 1, 0, 8)
        load_scales(w1s[1], w1_scales[:, :, 512:1024])
        load_words(xw, x_words, 1, 0, 8)
        load_scales(xs[1], x_scales[:, :, 512:1024])
        load_scales(w2s, w2_scales, nc.gpsimd)
        for a, b in ((0, 1024), (1024, 2048), (2048, 4096)):
            load_w2(a, b)
            load_y(0, a, b)
        for a in (0, 2048):
            load_y(1, a, a + 2048)

        def mm1(ps, h, g2, t, g):
            nc.tensor.matmul_mx(
                out=ps[:],
                lhsT=w1[g2][:, g, t * 256:(t + 1) * 256].bitcast(FP4X4),
                lhsT_scale=w1s[g2][:, g, t * 128:(t + 1) * 128],
                rhs=xw[h][:, g, :].bitcast(FP4X4),
                rhs_scale=xs[h][:, g, :],
                start=(g == 0), stop=(g == 7))

        acc = {}

        def begin_group(h, g2):
            acc[(h, g2)] = [work.tile([128, 4, 64], F32, name=s, tag=s) for s in ("asum", "amax")] + [
                work.tile([128, 4, 64], BF16, name="un", tag="un", bufs=3, align_bytes=64)]

        def silu(ps, h, g2, t):
            a = work.tile([128, 512], F32, name="a", tag="a", bufs=4)
            r = 64 + 4 * g2 + t
            nc.scalar.activation(out=a[:], in_=ps[:], func=ACT.Silu, bias=cst[:, r:r + 1])
            return a

        def reduce(a, h, g2, t):
            asum, amax, un = acc[(h, g2)]
            av = a[:].rearrange("p (i j) -> p i j", j=8)
            nc.vector.tensor_reduce(out=amax[:, t, :], in_=av, axis=AX.X, op=ALU.max)
            if (h, g2) == (0, 0):
                s4 = work.tile([128, 64, 4], F32, name="s4", tag="s4")
                s2 = work.tile([128, 64, 2], F32, name="s2", tag="s2")
                nc.gpsimd.tensor_tensor(out=s4[:], in0=av[:, :, 0:4], in1=av[:, :, 4:8], op=ALU.add)
                nc.gpsimd.tensor_tensor(out=s2[:], in0=s4[:, :, 0:2], in1=s4[:, :, 2:4], op=ALU.add)
                nc.gpsimd.tensor_tensor(out=asum[:, t, :], in0=s2[:, :, 0], in1=s2[:, :, 1], op=ALU.add)
            else:
                nc.vector.tensor_reduce(out=asum[:, t, :], in_=av, axis=AX.X, op=ALU.add)
            r = 80 + 4 * g2 + t
            nc.vector.tensor_scalar(out=amax[:, t, :], in0=amax[:, t, :], scalar1=cst[:, r:r + 1], scalar2=None, op0=ALU.mult)

        def mix(h, g2, t):
            asum, amax, un = acc[(h, g2)]
            r = 72 + 4 * g2 + t
            nc.vector.scalar_tensor_tensor(out=un[:, t, :], in0=asum[:, t, :], scalar=cst[:, r:r + 1], in1=amax[:, t, :],
                                           op0=ALU.mult, op1=ALU.add)

        ring = [0]

        def next_bank(shape=(128, 512)):
            ring[0] += 1
            return bank((ring[0] - 1) % 4, shape)

        def group_permute(h, g2):
            un = acc[(h, g2)][2]
            ps = next_bank((128, 4, 64))
            for t in range(4):
                for s in range(4):
                    nc.tensor.matmul(ps[:, t, :], lhsT=sel[:, t, 96 - 32 * s:224 - 32 * s], rhs=un[:, s, :],
                                     start=(s == 0), stop=(s == 3))
            return ps

        codes = {}

        def group_quant(h, g2, ps):
            ub = work.tile([128, 64, 2, 4], BF16, name="ub", tag="ub", align_bytes=64)
            nc.scalar.activation(out=ub[:], in_=ps[:].rearrange("p t i -> p i t").unsqueeze(2).to_broadcast([128, 64, 2, 4]), func=ACT.Copy)
            uc = keep.tile([128, 128], U32, name="uc%d%d" % (h, g2), align_bytes=64)
            us = keep.tile([128, 128], U8, name="us%d%d" % (h, g2), align_bytes=64)
            nc.vector.quantize_mx(out=uc[:].bitcast(FP8X4), scales=us[:], in_=ub[:].rearrange("p i r t -> p (i r t)"))
            codes[(h, g2)] = (uc, us)

        def zmm(h, n):
            zs = []
            for part in range(2):
                z = next_bank()
                for ct in range(4):
                    col = part * 4096 + n * 512 + ct * 128
                    for g2 in range(2):
                        uc, us = codes[(h, g2)]
                        nc.tensor.matmul_mx(
                            out=z[:, ct * 128:(ct + 1) * 128],
                            lhsT=w2[:, g2, 2 * col:2 * col + 256].bitcast(FP4X4),
                            lhsT_scale=w2s[:, g2, col:col + 128],
                            rhs=uc[:].bitcast(FP8X4),
                            rhs_scale=us[:],
                            start=(g2 == 0), stop=(g2 == 1))
                zs.append(z)
            return zs

        def evac(zs, n, part):
            r = work.tile([128, 4, 128], F32, name="zt%d" % part, tag="zt%d" % part, align_bytes=64)
            for ct in range(4):
                j = 32 * part + 4 * n + ct
                if part == 0:
                    nc.scalar.activation(out=r[:, ct, :], in_=zs[0][:, ct * 128:(ct + 1) * 128], func=ACT.Tanh,
                                         bias=cst[:, j:j + 1], scale=0.5)
                else:
                    nc.scalar.activation(out=r[:, ct, :], in_=zs[1][:, ct * 128:(ct + 1) * 128], func=ACT.Identity,
                                         bias=cst[:, j:j + 1])
            return r

        def turn(zt, n, part):
            b = bank(4 + 2 * part + n % 2)
            for ct in range(4):
                nc.tensor.transpose(b[:, ct * 128:(ct + 1) * 128], zt[:, ct, :], idf[:])
            return b

        def halve(gt):
            flat = gt[:].rearrange("p t i -> p (t i)")
            nc.scalar.activation(out=flat, in_=flat, func=ACT.Identity, bias=half[:], scale=0.5)

        def product(o, gate, h, n):
            c0 = (n % 4) * 512
            nc.vector.tensor_tensor(out=o, in0=ys[h][n // 4][:, :, c0:c0 + 512],
                                    in1=gate[:].unsqueeze(1).to_broadcast([128, 4, 512]), op=ALU.mult)

        def shift_copy(shift, i):
            ss = work.tile([128, 512], F32, name="ss", tag="ss", bufs=3, align_bytes=64)
            nc.scalar.activation(out=ss[:], in_=shift[:], func=ACT.Copy)
            return ss

        def store(src, i, a, b, c0, c1):
            h = i // 8
            nc.sync.dma_start(out=rows(out, h)[:, a:b, c0:c1], in_=src)

        def add_v(o, shift, a, b):
            nc.vector.tensor_tensor(out=o[:, a:b, :], in0=o[:, a:b, :],
                                    in1=shift[:].unsqueeze(1).to_broadcast([128, b - a, 512]), op=ALU.add)

        def add_g(o, ss, a, b):
            for j in range(a, b):
                nc.gpsimd.tensor_tensor(out=o[:, j, :], in0=o[:, j, :], in1=ss[:], op=ALU.add)

        def finish_chunk(pair, o, shift, ss, i):
            c0 = (i % 8) * 512
            add_v(o, shift, 0, J_V[i])
            add_g(o, ss, J_V[i], 4)
            for j in (0, 2):
                if i == 14:
                    store(o[:, j:j + 2, :], i, j, j + 2, c0, c0 + 512)
                elif i % 2:
                    store(pair[:, j:j + 2, :], i, j, j + 2, c0 - 512, c0 + 512)

        first = [bank(t) for t in range(4)]
        for g in range(8):
            for t in range(4):
                mm1(first[t], 0, 0, t, g)
            if g == 5:
                bt = bank(7, (128, 128), BF16)
                nc.tensor.transpose(bt[:], vr[:], idb[:])
                nc.vector.tensor_copy(out=cst[:], in_=bt[:, 0:88])
                nc.vector.tensor_scalar(out=cst[:, 0:32], in0=cst[:, 0:32], scalar1=0.5, scalar2=None, op0=ALU.mult)
                nc.vector.tensor_scalar(out=cst[:, 72:80], in0=cst[:, 72:80], scalar1=0.125, scalar2=None, op0=ALU.mult)
        begin_group(0, 0)
        for t in range(4):
            reduce(silu(first[t], 0, 0, t), 0, 0, t)

        begin_group(0, 1)
        for t in range(4):
            ps = bank(4 + t)
            for g in range(8):
                mm1(ps, 0, 1, t, g)
            a = silu(ps, 0, 1, t)
            reduce(a, 0, 1, t)
            if t:
                mix(0, 1, t - 1)
            if t == 2:
                for s in range(4):
                    mix(0, 0, s)
        mix(0, 1, 3)

        def stage1_b(k):
            g2, t = divmod(k, 4)
            if t == 0:
                begin_group(1, g2)
            ps = next_bank()
            for g in range(8):
                mm1(ps, 1, g2, t, g)
            return ps

        def post(k, ps):
            return silu(ps, 1, *divmod(k, 4))

        ps0 = stage1_b(0)
        a0 = post(0, ps0)
        pm = group_permute(0, 0)
        pm2 = group_permute(0, 1)
        group_quant(0, 0, pm)
        group_quant(0, 1, pm2)
        reduce(a0, 1, 0, 0)
        mix(1, 0, 0)

        items = [(h, n) for h in range(2) for n in range(8)]
        zs = {0: zmm(0, 0)}
        gts = {0: evac(zs[0], 0, 0)}
        halve(gts[0])
        sts = {0: evac(zs[0], 0, 1)}
        zs[1] = zmm(0, 1)
        silus = []
        ready = None
        for i, (h, n) in enumerate(items):
            if i:
                shift = turn(sts[i - 1], items[i - 1][1], 1)
            gate = turn(gts[i], n, 0)
            if i == 7 and 8 not in zs:
                zs[8] = zmm(*items[8])
            if i:
                ss = shift_copy(shift, i - 1)
            if i + 1 < 16:
                gts[i + 1] = evac(zs[i + 1], items[i + 1][1], 0)
                sts[i + 1] = evac(zs[i + 1], items[i + 1][1], 1)
                halve(gts[i + 1])
            new = [(j, stage1_b(j)) for j in ST1_B[i]]
            if ready == 0:
                pm = group_permute(1, 0)
            if i + 2 < 16 and (i != 6 or (1, 1) in codes):
                zs[i + 2] = zmm(*items[i + 2])
            if i % 2 == 0:
                pair = big([128, 4, 1024], F32, "pair")
            o = pair[:, :, (i % 2) * 512:(i % 2) * 512 + 512]
            product(o, gate, h, n)
            for j, a in silus:
                reduce(a, 1, *divmod(j, 4))
            last = silus and silus[-1][0] == 7
            if last:
                mix(1, 1, 3)
                pm = group_permute(1, 1)
            if i:
                finish_chunk(*pend, shift, ss, i - 1)
            if last:
                group_quant(1, 1, pm)
            for j, a in silus:
                if j != 7:
                    mix(1, *divmod(j, 4))
            if ready == 0:
                group_quant(1, 0, pm)
                ready = None
            if silus and silus[-1][0] in (3, 4) and (1, 0) not in codes:
                ready = 0
            silus = [(j, post(j, ps)) for j, ps in new]
            pend = (pair, o)
        shift = turn(sts[15], 7, 1)
        for a, b in ((0, 2), (2, 3), (3, 4)):
            add_v(o, shift, a, b)
            store(o[:, a:b, :], 15, a, b, 3584, 4096)
